import numpy as np
import ml_dtypes


def mxq(x, axis, fmt="e4m3"):
    dtype, down = {"e4m3": (ml_dtypes.float8_e4m3fn, 7), "e5m2": (ml_dtypes.float8_e5m2, 14)}[fmt]
    v = np.moveaxis(np.asarray(x, np.float32).astype(ml_dtypes.bfloat16).astype(np.float64), axis, -1)
    blocks = v.reshape(v.shape[:-1] + (-1, 32))
    amax = np.abs(blocks).max(-1, keepdims=True)
    byte = np.maximum(np.where(amax > 0, np.frexp(amax)[1] - 1 + 127, 0) - down, 1)
    scale = np.exp2(byte - 127.0)
    codes = (blocks / scale).astype(np.float32).astype(dtype).astype(np.float64)
    return np.moveaxis((codes * scale).reshape(v.shape), -1, axis)


WIDE = False


def mx_kscale(k):
    if not WIDE:
        return np.ones(k)
    levels = np.array([10, -10, 5, -5, 0])
    if k % 512:
        return np.exp2(np.random.permutation(np.resize(levels, k // 32))).repeat(32)
    a = np.empty((k // 512, 16))
    for p in range(k // 512):
        a[p, :8] = np.random.permutation(np.resize(levels, 8))
        for g in range(8):
            far = levels[np.abs(levels - a[p, g]) >= 10]
            a[p, g + 8] = far[np.random.randint(len(far))]
    return np.exp2(a.ravel()).repeat(32)


BF16 = ml_dtypes.bfloat16


def bf(x):
    return np.asarray(x, np.float32).astype(BF16)


def f64(x):
    return np.asarray(x).astype(np.float64)


E2M1 = np.array([0.0, 0.5, 1.0, 1.5, 2.0, 3.0, 4.0, 6.0, -0.0, -0.5, -1.0, -1.5, -2.0, -3.0, -4.0, -6.0])


def pack_weight(w, fmt):
    k, n = w.shape
    w = f64(bf(w)).reshape(k // 32, 32, n)
    amax = np.abs(w).max(1)
    if fmt == "e4m3":
        byte = np.frexp(amax)[1] - 1 + 127 - 7
    else:
        mant, ex = np.frexp(amax / 6.0)
        byte = np.where(mant > 0.5, ex, ex - 1) + 127
    byte = np.clip(np.where(amax > 0, byte, 1), 1, 254)
    scaled = (w * np.exp2(127.0 - byte)[:, None, :]).reshape(k, n).astype(np.float32)
    by_word = np.ascontiguousarray(scaled.reshape(k // 512, 128, 4, n).transpose(0, 1, 3, 2))
    if fmt == "e4m3":
        words = by_word.astype(ml_dtypes.float8_e4m3fn).view(np.uint8)
    else:
        c = by_word.astype(ml_dtypes.float4_e2m1fn).view(np.uint8) & 0xF
        words = c[..., 0::2] | (c[..., 1::2] << 4)
    return np.ascontiguousarray(words), np.ascontiguousarray(byte.astype(np.uint8).reshape(k // 512, 16, n))


def unpack_weight(words, scales, fmt):
    g, p, n, _ = words.shape
    if fmt == "e4m3":
        vals = np.ascontiguousarray(words).view(ml_dtypes.float8_e4m3fn).astype(np.float64)
    else:
        nib = np.empty((g, p, n, 4), np.uint8)
        nib[..., 0::2] = words & 0xF
        nib[..., 1::2] = words >> 4
        vals = E2M1[nib]
    vals = vals * np.repeat(np.exp2(scales.astype(np.float64) - 127.0), 8, axis=1)[..., None]
    return vals.transpose(0, 1, 3, 2).reshape(g * 512, n)
def pack4(w):
    words, scales = pack_weight(w, "e2m1")
    return words.reshape(words.shape[0], 128, -1), scales


def unpack4(words, scales):
    return unpack_weight(words.reshape(words.shape[0], 128, -1, 2), scales, "e2m1")


M, K, N, R, Q = 1024, 1536, 1024, 2048, 512


def draw0():
    s, t, u = mx_kscale(K), mx_kscale(N), mx_kscale(M)
    words, scales = pack4(np.random.standard_normal((N, R)) / np.sqrt(N) / t[:, None])
    return {"x": bf(np.random.standard_normal((M, K)) * s * u[:, None]),
            "prop": bf(np.random.standard_normal((K, N)) / np.sqrt(K) / s[:, None] * t),
            "y": bf(np.random.standard_normal((M, N)) * u[:, None] * t),
            "eof_words": words,
            "eof_scales": scales,
            "z": bf(np.random.standard_normal((Q, M)) / np.sqrt(M) / u),
            "prior": bf(np.random.standard_normal((Q, N)) * t),
            "keep": bf(np.random.uniform(0.6, 0.95, N))}


def core(x, prop, y, eof_words, eof_scales, z, prior, keep):
    forecast = mxq(f64(x), 1, "e4m3") @ mxq(f64(prop), 0, "e4m3")
    err = f64(y) - forecast
    maps = mxq(err, 1, "e4m3") @ unpack4(eof_words, eof_scales)
    fresh = mxq(f64(z), 1, "e4m3") @ mxq(err, 0, "e4m3")
    cov = f64(keep) * f64(prior) + fresh
    return maps, cov


def e4m3fn_bytes(y):
    return np.clip(np.asarray(y, np.float64), -448.0, 448.0).astype(np.float32).astype(ml_dtypes.float8_e4m3fn).view(np.uint8)


def e4m3fn_values(b):
    return np.asarray(b, np.uint8).view(ml_dtypes.float8_e4m3fn).astype(np.float64)


def setup_inputs():
    d = draw0()
    x0 = np.asarray(d['z']).astype(np.float64)
    s = (np.max(np.abs(x0), axis=(0,), keepdims=True) / 448.0).astype(np.float32)
    out = {}
    for k, v in d.items():
        if k == 'z':
            out['z_bytes'] = e4m3fn_bytes(x0 / s.astype(np.float64))
            out['z_scale'] = s
        else:
            out[k] = v
    return out


def reference(x, prop, y, eof_words, eof_scales, z_bytes, z_scale, prior, keep):
    return core(x, prop, y, eof_words, eof_scales, e4m3fn_values(z_bytes) * z_scale.astype(np.float64), prior, keep)

@@ -1,0 +1,445 @@
+from contextlib import ExitStack
+
+import concourse.mybir as mybir
+from concourse.masks import make_identity
+
+M, K, N, R, Q = 1024, 1536, 1024, 2048, 512
+FLOPS = 2 * (M * K * N + M * N * R + Q * M * N)
+
+F32 = mybir.dt.float32
+BF16 = mybir.dt.bfloat16
+U32 = mybir.dt.uint32
+I32 = mybir.dt.int32
+U8 = mybir.dt.uint8
+FP8 = mybir.dt.float8_e4m3fn
+FP8X4 = mybir.dt.float8_e4m3fn_x4
+FP4X4 = mybir.dt.float4_e2m1fn_x4
+ALU = mybir.AluOpType
+
+P = 128
+BANK = 512
+KP = K // 512
+PAIRS = 4
+V_COLS = 336
+
+
+def tile_lim_error_update_s8_kernel(tc, x, prop, y, eof_words, eof_scales, z_bytes, z_scale, prior, keep, maps, cov):
+    nc = tc.nc
+    with ExitStack() as ctx:
+        keepers = ctx.enter_context(tc.tile_pool(name="keepers", bufs=1))
+        work = ctx.enter_context(tc.tile_pool(name="work", bufs=2))
+        psum = ctx.enter_context(tc.psum_pool(name="psum", bufs=8))
+
+        def kept(name, shape, dt):
+            return keepers.tile(shape, dt, name=name, align_bytes=64)
+
+        def bank(name="bank"):
+            return psum.tile([P, BANK], F32, name="bank")
+
+        def big():
+            return work.tile([P, 2048], F32, name="big", bufs=7, align_bytes=64)
+
+        def grouped():
+            return work.tile([P, 2048], BF16, name="grouped", bufs=7, align_bytes=64)
+
+        ident = kept("ident", [P, P], F32)
+        make_identity(nc, ident[:])
+        ones = kept("ones", [P, P], BF16)
+        keep_row = kept("keep_row", [P, N], BF16)
+        e_scale = kept("e_scale", [P, 2, R], U8)
+
+        x_view = x.rearrange("(g p t) k -> g p t k", g=2, t=4)
+        y_view = y.rearrange("(g p t) n -> g p t n", g=2, t=4)
+        maps_view = maps.rearrange("(g p t) r -> g p t r", g=2, t=4)
+        prop_view = prop.rearrange("(c p j) n -> c p j n", p=P, j=4)
+        prior_view = prior.rearrange("(p a) n -> p a n", a=4)
+        cov_view = cov.rearrange("(p a) n -> p a n", a=4)
+
+        x_raw, y_raw, prop_raw = {}, {}, {}
+        x_codes = [kept("x_codes%d" % i, [P, KP, 256], U32) for i in range(PAIRS)]
+        x_scl = [kept("x_scl%d" % i, [P, KP, 256], U8) for i in range(PAIRS)]
+        p_codes = [[kept("p_codes%d%d" % (c, h), [P, 512], U32) for h in range(2)] for c in range(KP)]
+        p_scl = [[kept("p_scl%d%d" % (c, h), [P, 512], U8) for h in range(2)] for c in range(KP)]
+        err = [[kept("err%d%d" % (g, h), [P, 4, 512], BF16) for h in range(2)] for g in range(2)]
+        et_codes = [kept("et_codes%d" % i, [P, 2, 256], U32) for i in range(PAIRS)]
+        et_scl = [kept("et_scl%d" % i, [P, 2, 256], U8) for i in range(PAIRS)]
+        em_codes = [[kept("em_codes%d%d" % (g, h), [P, 512], U32) for h in range(2)] for g in range(2)]
+        em_scl = [[kept("em_scl%d%d" % (g, h), [P, 512], U8) for h in range(2)] for g in range(2)]
+        z_codes = [kept("z_codes%d" % g, [P, Q], U32) for g in range(2)]
+        z_scl = [kept("z_scl%d" % g, [P, Q], U8) for g in range(2)]
+        e_words = kept("e_words", [P, 2, 2 * R], U8)
+        z_in = kept("z_in", [P, 4, M], U8)
+        z_sc = kept("z_sc", [P, 2, 4], F32)
+        z_wide = kept("z_wide", [P, 4, M], BF16)
+        prior_sb = kept("prior_sb", [P, 4, N], BF16)
+        keep_all = kept("keep_all", [P, N], F32)
+
+        def load(out, in_):
+            nc.sync.dma_start(out=out, in_=in_)
+
+        def load_x(i):
+            g, h = divmod(i, 2)
+            x_raw[i] = work.tile([P, 2, K], BF16, name="x_raw", bufs=3, align_bytes=64)
+            load(x_raw[i][:], x_view[g][:, 2 * h : 2 * h + 2, :])
+
+        def load_y(i):
+            g, h = divmod(i, 2)
+            if h == 0:
+                y_raw[g] = kept("y_raw%d" % g, [P, 4, N], BF16)
+            load(y_raw[g][:, 2 * h : 2 * h + 2, :], y_view[g][:, 2 * h : 2 * h + 2, :])
+
+        def load_prop(c, h):
+            if c not in prop_raw:
+                prop_raw[c] = big()[:].bitcast(BF16).rearrange("p (j n) -> p j n", j=4)
+            cols = slice(512 * h, 512 * h + 512)
+            load(prop_raw[c][:, :, cols], prop_view[c][:, :, cols])
+
+        def load_e():
+            load(e_words[:].bitcast(I32), eof_words.rearrange("g p b -> p g b").bitcast(I32))
+
+        def load_e_scales():
+            for q in range(4):
+                load(
+                    e_scale[32 * q : 32 * q + 4, :, :].bitcast(I32),
+                    eof_scales[:, 4 * q : 4 * q + 4, :].rearrange("g q n -> q g n").bitcast(I32),
+                )
+
+        def prop_interleave(c, h):
+            t = grouped()
+            dst = t[:].rearrange("p (n j) -> p n j", j=4)
+            src = prop_raw[c][:, :, 512 * h : 512 * h + 512].rearrange("p j n -> p n j")
+            nc.scalar.copy(out=dst[:, V_COLS:, :], in_=src[:, V_COLS:, :])
+            nc.vector.tensor_copy(out=dst[:, :V_COLS, :], in_=src[:, :V_COLS, :])
+            return t
+
+        def quantize(codes, scl, t):
+            nc.vector.quantize_mx(out=codes.bitcast(FP8X4), scales=scl, in_=t)
+
+        def x_transpose(i):
+            out = []
+            words = x_raw[i][:].bitcast(F32)
+            for c in range(KP):
+                b = bank()
+                v = b[:].rearrange("p (u t m) -> p u t m", u=2, t=2)
+                for u in range(2):
+                    for t in range(2):
+                        nc.tensor.transpose(v[:, u, t, :], words[:, t, 256 * c + u : 256 * (c + 1) : 2], ident[:])
+                out.append(b)
+            return out
+
+        def pull_pairs(b):
+            t = grouped()
+            nc.scalar.copy(
+                out=t[:, :1024].bitcast(F32).rearrange("p (m u) -> p m u", u=2),
+                in_=b[:].rearrange("p (u m) -> p m u", u=2),
+            )
+            return t
+
+        def x_pull(banks):
+            return [pull_pairs(b) for b in banks]
+
+        def x_quant(i, tiles):
+            for c in range(KP):
+                quantize(x_codes[i][:, c, :], x_scl[i][:, c, :], tiles[c][:, :1024])
+
+        def forecast_pass(i, t, h, c, b):
+            cols = slice(128 * t, 128 * t + 128)
+            nc.tensor.matmul_mx(
+                out=b[:],
+                lhsT=x_codes[i][:, c, cols].bitcast(FP8X4),
+                lhsT_scale=x_scl[i][:, c, cols],
+                rhs=p_codes[c][h][:].bitcast(FP8X4),
+                rhs_scale=p_scl[c][h][:],
+                start=(c == 0),
+                stop=(c == KP - 1),
+            )
+
+        def forecast(i, t, h):
+            b = bank()
+            for c in range(KP):
+                forecast_pass(i, t, h, c, b)
+            return b
+
+        def subtract(i, t, h, b):
+            g, tp = divmod(i, 2)
+            tt = 2 * tp + t
+            view = "m (p u e) -> m u p e"
+            nc.vector.tensor_tensor(
+                out=err[g][h][:, tt, :].rearrange("m (u p e) -> m u p e", u=2, e=2),
+                in0=y_raw[g][:, tt, 512 * h : 512 * h + 512].rearrange(view, u=2, e=2),
+                in1=b[:].rearrange(view, u=2, e=2),
+                op=ALU.subtract,
+            )
+
+        def err_transpose(i, t):
+            g, tp = divmod(i, 2)
+            b = bank()
+            v = b[:].rearrange("p (u h m) -> p u h m", u=2, h=2)
+            for h in range(2):
+                words = err[g][h][:, 2 * tp + t, :].bitcast(F32)
+                for u in range(2):
+                    nc.tensor.transpose(v[:, u, h, :], words[:, 128 * u : 128 * u + 128], ident[:])
+            return b
+
+        def err_t_quant(i, t, tile):
+            quantize(et_codes[i][:, t, :], et_scl[i][:, t, :], tile[:, :1024])
+
+        def err_m_interleave(g, h):
+            t = grouped()
+            nc.vector.tensor_copy(
+                out=t[:].rearrange("p (n j) -> p n j", j=4), in_=err[g][h][:].rearrange("p j n -> p n j")
+            )
+            return t
+
+        def err_m_quant(g, h, t):
+            quantize(em_codes[g][h][:], em_scl[g][h][:], t[:])
+
+        def maps_tile(i, t, r):
+            b = bank()
+            for h in range(2):
+                k = slice(128 * h, 128 * h + 128)
+                nc.tensor.matmul_mx(
+                    out=b[:],
+                    lhsT=et_codes[i][:, t, k].bitcast(FP8X4),
+                    lhsT_scale=et_scl[i][:, t, k],
+                    rhs=e_words[:, h, 1024 * r : 1024 * r + 1024].bitcast(FP4X4),
+                    rhs_scale=e_scale[:, h, 512 * r : 512 * r + 512],
+                    start=(h == 0),
+                    stop=(h == 1),
+                )
+            return b
+
+        def maps_unit(i, t, on_vector, pieces=1):
+            g, tp = divmod(i, 2)
+            o = big()
+            n = 4 // pieces
+            for r in range(4):
+                b = maps_tile(i, t, r)
+                cols = slice(512 * r, 512 * r + 512)
+                if r in on_vector:
+                    nc.vector.tensor_copy(out=o[:, cols], in_=b[:])
+                else:
+                    nc.scalar.copy(out=o[:, cols], in_=b[:])
+                if (r + 1) % n == 0:
+                    c = slice(512 * (r + 1 - n), 512 * (r + 1))
+                    nc.sync.dma_start(out=maps_view[g][:, 2 * tp + t, c], in_=o[:, c])
+
+        def z_widen(a):
+            nc.scalar.copy(out=z_wide[:, a, :], in_=z_in[:, a, :].bitcast(FP8))
+
+        def z_transpose(g, ap):
+            b = bank()
+            v = b[:].rearrange("p (u a q) -> p u a q", u=2, a=2)
+            for u in range(2):
+                for a in range(2):
+                    words = z_wide[:, 2 * ap + a, :].bitcast(F32)
+                    nc.tensor.transpose(v[:, u, a, :], words[:, 256 * g + u : 256 * (g + 1) : 2], ident[:])
+            return b
+
+        def z_pull(g, ap, b, t):
+            nc.vector.tensor_tensor(
+                out=t[:, 1024 * ap : 1024 * ap + 1024].rearrange("p (q u e) -> p q u e", u=2, e=2),
+                in0=b[:].bitcast(BF16).rearrange("p (u q e) -> p q u e", u=2, e=2),
+                in1=z_sc[:, g, :].rearrange("p (u e) -> p u e", u=2).unsqueeze(1).to_broadcast([P, 256, 2, 2]),
+                op=ALU.mult,
+            )
+
+        def keep_spread():
+            for h in range(2):
+                b = bank()
+                cols = slice(512 * h, 512 * h + 512)
+                nc.tensor.matmul(b[:], ones[:], keep_row[:, cols], start=True, stop=True)
+                nc.scalar.copy(out=keep_all[:, cols], in_=b[:])
+
+        cov_sb = {}
+
+        def keep_prior(a):
+            if a % 2 == 0:
+                cov_sb[a // 2] = big()
+            nc.vector.tensor_tensor(
+                out=cov_sb[a // 2][:, 1024 * (a % 2) : 1024 * (a % 2) + 1024],
+                in0=prior_sb[:, a, :], in1=keep_all[:], op=ALU.mult,
+            )
+
+        def cov_tile(a, h):
+            b = bank()
+            qs = slice(128 * a, 128 * a + 128)
+            for g in range(2):
+                nc.tensor.matmul_mx(
+                    out=b[:],
+                    lhsT=z_codes[g][:, qs].bitcast(FP8X4),
+                    lhsT_scale=z_scl[g][:, qs],
+                    rhs=em_codes[g][h][:].bitcast(FP8X4),
+                    rhs_scale=em_scl[g][h][:],
+                    start=(g == 0),
+                    stop=(g == 1),
+                )
+            lo = 1024 * (a % 2) + 512 * h
+            view = "q (p u e) -> q p u e"
+            dst = cov_sb[a // 2][:, lo : lo + 512]
+            nc.vector.tensor_tensor(
+                out=dst.rearrange(view, u=2, e=2),
+                in0=b[:].rearrange("q (u p e) -> q p u e", u=2, e=2),
+                in1=dst.rearrange(view, u=2, e=2),
+                op=ALU.add,
+            )
+
+        def cov_store(a):
+            lo = 1024 * (a % 2)
+            nc.sync.dma_start(out=cov_view[:, a, :], in_=cov_sb[a // 2][:, lo : lo + 1024])
+
+        with tc.manual_schedule():
+            nc.vector.memset(e_scale[:].rearrange("p g n -> p (g n)").bitcast(I32), 0)
+            nc.vector.memset(keep_row[:], 0.0)
+            nc.vector.memset(ones[:], 1.0)
+            load_x(0)
+            load_prop(0, 0)
+            load_prop(1, 0)
+            load_x(1)
+            load_prop(2, 0)
+            load_prop(0, 1)
+            load_prop(1, 1)
+            load_prop(2, 1)
+            load_y(0)
+            load_x(2)
+            load_y(1)
+            load(z_in[:], z_bytes.rearrange("(p a) m -> p a m", a=4))
+            load(z_sc[:], z_scale.rearrange("o (g p t) -> p (o g) t", g=2, t=4))
+            load(keep_row[0:1, :], keep.rearrange("(o n) -> o n", o=1))
+            load_e()
+            load_e_scales()
+            load_y(2)
+
+            def p_quant(c, h, t):
+                quantize(p_codes[c][h][:], p_scl[c][h][:], t[:])
+
+            def x_q1(i, c, t):
+                quantize(x_codes[i][:, c, :], x_scl[i][:, c, :], t[:, :1024])
+
+            xb = x_transpose(0)
+            load_x(3)
+            load_y(3)
+            load(prior_sb[:], prior_view)
+            x0 = [pull_pairs(xb[0])]
+            p00 = prop_interleave(0, 0)
+            x0 += [pull_pairs(b) for b in xb[1:]]
+            x_q1(0, 0, x0[0])
+            p_quant(0, 0, p00)
+            p10 = prop_interleave(1, 0)
+            x_q1(0, 1, x0[1])
+            x_q1(0, 2, x0[2])
+            xb = x_transpose(1)
+            p_quant(1, 0, p10)
+            x1 = [pull_pairs(xb[0])]
+            p20 = prop_interleave(2, 0)
+            x1 += [pull_pairs(b) for b in xb[1:]]
+            f00 = [bank(), bank()]
+            for c in range(2):
+                for t in range(2):
+                    forecast_pass(0, t, 0, c, f00[t])
+            x_q1(1, 0, x1[0])
+            p_quant(2, 0, p20)
+            for t in range(2):
+                forecast_pass(0, t, 0, 2, f00[t])
+            x_q1(1, 1, x1[1])
+            p01 = prop_interleave(0, 1)
+            x_q1(1, 2, x1[2])
+            f10 = [forecast(1, t, 0) for t in range(2)]
+            p_quant(0, 1, p01)
+            p11 = prop_interleave(1, 1)
+            subtract(0, 0, 0, f00[0])
+            p_quant(1, 1, p11)
+            f01 = [bank(), bank()]
+            for c in range(2):
+                for t in range(2):
+                    forecast_pass(0, t, 1, c, f01[t])
+            p21 = prop_interleave(2, 1)
+            subtract(0, 1, 0, f00[1])
+            p_quant(2, 1, p21)
+            xb = x_transpose(2)
+            x2 = [pull_pairs(b) for b in xb]
+            for t in range(2):
+                forecast_pass(0, t, 1, 2, f01[t])
+            subtract(1, 0, 0, f10[0])
+            subtract(1, 1, 0, f10[1])
+            f11 = [forecast(1, t, 1) for t in range(2)]
+            for t in range(2):
+                subtract(0, t, 1, f01[t])
+            for c in range(3):
+                x_q1(2, c, x2[c])
+            z_widen(0)
+            z_widen(1)
+            for t in range(2):
+                subtract(1, t, 1, f11[t])
+            eb = [err_transpose(0, t) for t in range(2)]
+            e0 = [pull_pairs(b) for b in eb]
+            f20 = [forecast(2, t, 0) for t in range(2)]
+            mt = err_m_interleave(0, 0)
+            z_widen(2)
+            z_widen(3)
+            for t in range(2):
+                err_t_quant(0, t, e0[t])
+            eb = [err_transpose(1, t) for t in range(2)]
+            e1 = [pull_pairs(b) for b in eb]
+            err_m_quant(0, 0, mt)
+            for t in range(2):
+                subtract(2, t, 0, f20[t])
+            maps_unit(0, 0, (3,), 2)
+            for t in range(2):
+                err_t_quant(1, t, e1[t])
+            mt = err_m_interleave(0, 1)
+            zt = [grouped() for g in range(2)]
+            zb = [z_transpose(g, 0) for g in range(2)]
+            err_m_quant(0, 1, mt)
+            maps_unit(0, 1, (), 2)
+            for g in range(2):
+                z_pull(g, 0, zb[g], zt[g])
+            f21 = [forecast(2, t, 1) for t in range(2)]
+            for t in range(2):
+                subtract(2, t, 1, f21[t])
+            keep_spread()
+            xb = x_transpose(3)
+            x3 = [pull_pairs(b) for b in xb]
+            eb = [err_transpose(2, t) for t in range(2)]
+            for c in range(3):
+                x_q1(3, c, x3[c])
+            e2 = [pull_pairs(b) for b in eb]
+            keep_prior(0)
+            maps_unit(1, 0, (), 2)
+            for t in range(2):
+                err_t_quant(2, t, e2[t])
+            keep_prior(1)
+            f30 = [forecast(3, t, 0) for t in range(2)]
+            for t in range(2):
+                subtract(3, t, 0, f30[t])
+            f31 = [forecast(3, t, 1) for t in range(2)]
+            mt = err_m_interleave(1, 0)
+            for t in range(2):
+                subtract(3, t, 1, f31[t])
+            maps_unit(1, 1, (), 2)
+            err_m_quant(1, 0, mt)
+            zb = [z_transpose(g, 1) for g in range(2)]
+            eb = [err_transpose(3, t) for t in range(2)]
+            e3 = [pull_pairs(b) for b in eb]
+            for g in range(2):
+                z_pull(g, 1, zb[g], zt[g])
+            mt = err_m_interleave(1, 1)
+            for g in range(2):
+                quantize(z_codes[g][:], z_scl[g][:], zt[g][:])
+            maps_unit(2, 0, (), 2)
+            err_m_quant(1, 1, mt)
+            for t in range(2):
+                err_t_quant(3, t, e3[t])
+            maps_unit(2, 1, (), 2)
+            for a in range(2):
+                for h in range(2):
+                    cov_tile(a, h)
+                cov_store(a)
+            keep_prior(2)
+            keep_prior(3)
+            maps_unit(3, 0, (), 2)
+            for a in range(2, 4):
+                for h in range(2):
+                    cov_tile(a, h)
+                cov_store(a)
+            maps_unit(3, 1, (3,), 4)

@@ -20,6 +20,8 @@ P = 128
 BANK = 512
 KP = K // 512
 PAIRS = 4
+MAPS_ON_VECTOR = {}
+LAST = (3, 1)
 V_COLS = 336
 
 
@@ -40,11 +42,14 @@ def tile_lim_error_update_s8_kernel(tc, x, prop, y, eof_words, eof_scales, z_byt
             return work.tile([P, 2048], F32, name="big", bufs=7, align_bytes=64)
 
         def grouped():
-            return work.tile([P, 2048], BF16, name="grouped", bufs=7, align_bytes=64)
+            return work.tile([P, 2048], BF16, name="grouped", bufs=5, align_bytes=64)
+
+        def half():
+            return work.tile([P, 1024], BF16, name="half", bufs=7, align_bytes=64)
 
         ident = kept("ident", [P, P], F32)
         make_identity(nc, ident[:])
-        ones = kept("ones", [P, P], BF16)
+        ones = kept("ones", [P, BANK], BF16)
         keep_row = kept("keep_row", [P, N], BF16)
         e_scale = kept("e_scale", [P, 2, R], U8)
 
@@ -77,10 +82,11 @@ def tile_lim_error_update_s8_kernel(tc, x, prop, y, eof_words, eof_scales, z_byt
         def load(out, in_):
             nc.sync.dma_start(out=out, in_=in_)
 
-        def load_x(i):
+        def load_x(i, t):
             g, h = divmod(i, 2)
-            x_raw[i] = work.tile([P, 2, K], BF16, name="x_raw", bufs=3, align_bytes=64)
-            load(x_raw[i][:], x_view[g][:, 2 * h : 2 * h + 2, :])
+            if t == 0:
+                x_raw[i] = work.tile([P, 2, K], BF16, name="x_raw", bufs=3, align_bytes=64)
+            load(x_raw[i][:, t, :], x_view[g][:, 2 * h + t, :])
 
         def load_y(i):
             g, h = divmod(i, 2)
@@ -104,48 +110,56 @@ def tile_lim_error_update_s8_kernel(tc, x, prop, y, eof_words, eof_scales, z_byt
                     eof_scales[:, 4 * q : 4 * q + 4, :].rearrange("g q n -> q g n").bitcast(I32),
                 )
 
-        def prop_interleave(c, h):
-            t = grouped()
-            dst = t[:].rearrange("p (n j) -> p n j", j=4)
-            src = prop_raw[c][:, :, 512 * h : 512 * h + 512].rearrange("p j n -> p n j")
-            nc.scalar.copy(out=dst[:, V_COLS:, :], in_=src[:, V_COLS:, :])
-            nc.vector.tensor_copy(out=dst[:, :V_COLS, :], in_=src[:, :V_COLS, :])
-            return t
+        banks, tiles = {}, {}
 
         def quantize(codes, scl, t):
             nc.vector.quantize_mx(out=codes.bitcast(FP8X4), scales=scl, in_=t)
 
-        def x_transpose(i):
-            out = []
-            words = x_raw[i][:].bitcast(F32)
-            for c in range(KP):
-                b = bank()
-                v = b[:].rearrange("p (u t m) -> p u t m", u=2, t=2)
-                for u in range(2):
-                    for t in range(2):
-                        nc.tensor.transpose(v[:, u, t, :], words[:, t, 256 * c + u : 256 * (c + 1) : 2], ident[:])
-                out.append(b)
-            return out
+        def warm(n):
+            b = bank()
+            for k in range(n):
+                nc.tensor.matmul(b[:], ones[:, :P], ones[:], start=True, stop=True)
 
-        def pull_pairs(b):
-            t = grouped()
+        def prop_interleave(c, h):
+            t = tiles["prop", c, h] = grouped()
+            dst = t[:].rearrange("p (n j) -> p n j", j=4)
+            src = prop_raw[c][:, :, 512 * h : 512 * h + 512].rearrange("p j n -> p n j")
+            nc.scalar.copy(out=dst[:, V_COLS:, :], in_=src[:, V_COLS:, :])
+            nc.vector.tensor_copy(out=dst[:, :V_COLS, :], in_=src[:, :V_COLS, :])
+
+        def prop_quant(c, h):
+            quantize(p_codes[c][h][:], p_scl[c][h][:], tiles["prop", c, h][:])
+
+        def x_transpose(i):
+            for c in range(KP):
+                banks["x", i, c] = bank()
+            for t in range(2):
+                words = x_raw[i][:, t, :].bitcast(F32)
+                for c in range(KP):
+                    v = banks["x", i, c][:].rearrange("p (u t m) -> p u t m", u=2, t=2)
+                    for u in range(2):
+                        nc.tensor.transpose(v[:, u, t, :], words[:, 256 * c + u : 256 * (c + 1) : 2], ident[:])
+
+        def pull_words(b):
+            t = half()
             nc.scalar.copy(
-                out=t[:, :1024].bitcast(F32).rearrange("p (m u) -> p m u", u=2),
+                out=t[:].bitcast(F32).rearrange("p (m u) -> p m u", u=2),
                 in_=b[:].rearrange("p (u m) -> p m u", u=2),
             )
             return t
 
-        def x_pull(banks):
-            return [pull_pairs(b) for b in banks]
+        def x_pull(i, c):
+            tiles["x", i, c] = pull_words(banks["x", i, c])
 
-        def x_quant(i, tiles):
-            for c in range(KP):
-                quantize(x_codes[i][:, c, :], x_scl[i][:, c, :], tiles[c][:, :1024])
+        def x_quant(i, c):
+            quantize(x_codes[i][:, c, :], x_scl[i][:, c, :], tiles["x", i, c][:])
 
-        def forecast_pass(i, t, h, c, b):
+        def forecast_pass(i, t, h, c):
             cols = slice(128 * t, 128 * t + 128)
+            if c == 0:
+                banks["f", i, t, h] = bank()
             nc.tensor.matmul_mx(
-                out=b[:],
+                out=banks["f", i, t, h][:],
                 lhsT=x_codes[i][:, c, cols].bitcast(FP8X4),
                 lhsT_scale=x_scl[i][:, c, cols],
                 rhs=p_codes[c][h][:].bitcast(FP8X4),
@@ -154,292 +168,290 @@ def tile_lim_error_update_s8_kernel(tc, x, prop, y, eof_words, eof_scales, z_byt
                 stop=(c == KP - 1),
             )
 
-        def forecast(i, t, h):
-            b = bank()
-            for c in range(KP):
-                forecast_pass(i, t, h, c, b)
-            return b
+        def forecast0(h, c):
+            for t in range(2):
+                forecast_pass(0, t, h, c)
 
-        def subtract(i, t, h, b):
+        def forecast(i, h):
+            for t in range(2):
+                for c in range(KP):
+                    forecast_pass(i, t, h, c)
+
+        def subtract(i, h):
             g, tp = divmod(i, 2)
-            tt = 2 * tp + t
             view = "m (p u e) -> m u p e"
-            nc.vector.tensor_tensor(
-                out=err[g][h][:, tt, :].rearrange("m (u p e) -> m u p e", u=2, e=2),
-                in0=y_raw[g][:, tt, 512 * h : 512 * h + 512].rearrange(view, u=2, e=2),
-                in1=b[:].rearrange(view, u=2, e=2),
-                op=ALU.subtract,
-            )
+            for t in range(2):
+                tt = 2 * tp + t
+                nc.vector.tensor_tensor(
+                    out=err[g][h][:, tt, :].rearrange("m (u p e) -> m u p e", u=2, e=2),
+                    in0=y_raw[g][:, tt, 512 * h : 512 * h + 512].rearrange(view, u=2, e=2),
+                    in1=banks["f", i, t, h][:].rearrange(view, u=2, e=2),
+                    op=ALU.subtract,
+                )
 
-        def err_transpose(i, t):
+        def err_transpose(i):
             g, tp = divmod(i, 2)
-            b = bank()
-            v = b[:].rearrange("p (u h m) -> p u h m", u=2, h=2)
-            for h in range(2):
-                words = err[g][h][:, 2 * tp + t, :].bitcast(F32)
-                for u in range(2):
-                    nc.tensor.transpose(v[:, u, h, :], words[:, 128 * u : 128 * u + 128], ident[:])
-            return b
+            for t in range(2):
+                b = banks["e", i, t] = bank()
+                v = b[:].rearrange("p (u h m) -> p u h m", u=2, h=2)
+                for h in range(2):
+                    words = err[g][h][:, 2 * tp + t, :].bitcast(F32)
+                    for u in range(2):
+                        nc.tensor.transpose(v[:, u, h, :], words[:, 128 * u : 128 * u + 128], ident[:])
 
-        def err_t_quant(i, t, tile):
-            quantize(et_codes[i][:, t, :], et_scl[i][:, t, :], tile[:, :1024])
+        def err_pull(i):
+            for t in range(2):
+                tiles["e", i, t] = pull_words(banks["e", i, t])
 
-        def err_m_interleave(g, h):
-            t = grouped()
+        def err_quant(i):
+            for t in range(2):
+                quantize(et_codes[i][:, t, :], et_scl[i][:, t, :], tiles["e", i, t][:])
+
+        def month_interleave(g, h):
+            t = tiles["m", g, h] = grouped()
             nc.vector.tensor_copy(
                 out=t[:].rearrange("p (n j) -> p n j", j=4), in_=err[g][h][:].rearrange("p j n -> p n j")
             )
-            return t
 
-        def err_m_quant(g, h, t):
-            quantize(em_codes[g][h][:], em_scl[g][h][:], t[:])
+        def month_quant(g, h):
+            quantize(em_codes[g][h][:], em_scl[g][h][:], tiles["m", g, h][:])
 
-        def maps_tile(i, t, r):
-            b = bank()
-            for h in range(2):
-                k = slice(128 * h, 128 * h + 128)
-                nc.tensor.matmul_mx(
-                    out=b[:],
-                    lhsT=et_codes[i][:, t, k].bitcast(FP8X4),
-                    lhsT_scale=et_scl[i][:, t, k],
-                    rhs=e_words[:, h, 1024 * r : 1024 * r + 1024].bitcast(FP4X4),
-                    rhs_scale=e_scale[:, h, 512 * r : 512 * r + 512],
-                    start=(h == 0),
-                    stop=(h == 1),
-                )
-            return b
-
-        def maps_unit(i, t, on_vector, pieces=1):
+        def maps_half(i, t, j):
             g, tp = divmod(i, 2)
-            o = big()
-            n = 4 // pieces
-            for r in range(4):
-                b = maps_tile(i, t, r)
+            if ("o", i, t) not in tiles:
+                tiles["o", i, t] = big()
+            o = tiles["o", i, t]
+            for r in (2 * j, 2 * j + 1):
+                b = bank()
+                for h in range(2):
+                    k = slice(128 * h, 128 * h + 128)
+                    nc.tensor.matmul_mx(
+                        out=b[:],
+                        lhsT=et_codes[i][:, t, k].bitcast(FP8X4),
+                        lhsT_scale=et_scl[i][:, t, k],
+                        rhs=e_words[:, h, 1024 * r : 1024 * r + 1024].bitcast(FP4X4),
+                        rhs_scale=e_scale[:, h, 512 * r : 512 * r + 512],
+                        start=(h == 0),
+                        stop=(h == 1),
+                    )
                 cols = slice(512 * r, 512 * r + 512)
-                if r in on_vector:
+                if (i, t, r) in MAPS_ON_VECTOR:
                     nc.vector.tensor_copy(out=o[:, cols], in_=b[:])
                 else:
                     nc.scalar.copy(out=o[:, cols], in_=b[:])
-                if (r + 1) % n == 0:
-                    c = slice(512 * (r + 1 - n), 512 * (r + 1))
-                    nc.sync.dma_start(out=maps_view[g][:, 2 * tp + t, c], in_=o[:, c])
+                if (i, t) == LAST:
+                    nc.sync.dma_start(out=maps_view[g][:, 2 * tp + t, cols], in_=o[:, cols])
+            if (i, t) != LAST:
+                cols = slice(1024 * j, 1024 * j + 1024)
+                nc.sync.dma_start(out=maps_view[g][:, 2 * tp + t, cols], in_=o[:, cols])
 
         def z_widen(a):
             nc.scalar.copy(out=z_wide[:, a, :], in_=z_in[:, a, :].bitcast(FP8))
 
-        def z_transpose(g, ap):
-            b = bank()
-            v = b[:].rearrange("p (u a q) -> p u a q", u=2, a=2)
-            for u in range(2):
-                for a in range(2):
-                    words = z_wide[:, 2 * ap + a, :].bitcast(F32)
-                    nc.tensor.transpose(v[:, u, a, :], words[:, 256 * g + u : 256 * (g + 1) : 2], ident[:])
-            return b
+        def z_transpose(ap):
+            for g in range(2):
+                b = banks["z", g, ap] = bank()
+                v = b[:].rearrange("p (u a q) -> p u a q", u=2, a=2)
+                for u in range(2):
+                    for a in range(2):
+                        words = z_wide[:, 2 * ap + a, :].bitcast(F32)
+                        nc.tensor.transpose(v[:, u, a, :], words[:, 256 * g + u : 256 * (g + 1) : 2], ident[:])
 
-        def z_pull(g, ap, b, t):
-            nc.vector.tensor_tensor(
-                out=t[:, 1024 * ap : 1024 * ap + 1024].rearrange("p (q u e) -> p q u e", u=2, e=2),
-                in0=b[:].bitcast(BF16).rearrange("p (u q e) -> p q u e", u=2, e=2),
-                in1=z_sc[:, g, :].rearrange("p (u e) -> p u e", u=2).unsqueeze(1).to_broadcast([P, 256, 2, 2]),
-                op=ALU.mult,
-            )
+        def z_pull(ap):
+            for g in range(2):
+                if ("z", g) not in tiles:
+                    tiles["z", g] = grouped()
+                nc.vector.tensor_tensor(
+                    out=tiles["z", g][:, 1024 * ap : 1024 * ap + 1024].rearrange("p (q u e) -> p q u e", u=2, e=2),
+                    in0=banks["z", g, ap][:].bitcast(BF16).rearrange("p (u q e) -> p q u e", u=2, e=2),
+                    in1=z_sc[:, g, :].rearrange("p (u e) -> p u e", u=2).unsqueeze(1).to_broadcast([P, 256, 2, 2]),
+                    op=ALU.mult,
+                )
+
+        def z_quant():
+            for g in range(2):
+                quantize(z_codes[g][:], z_scl[g][:], tiles["z", g][:])
 
         def keep_spread():
             for h in range(2):
                 b = bank()
                 cols = slice(512 * h, 512 * h + 512)
-                nc.tensor.matmul(b[:], ones[:], keep_row[:, cols], start=True, stop=True)
+                nc.tensor.matmul(b[:], ones[:, :P], keep_row[:, cols], start=True, stop=True)
                 nc.scalar.copy(out=keep_all[:, cols], in_=b[:])
 
-        cov_sb = {}
+        def cov_half(a):
+            if ("c", a // 2) not in tiles:
+                tiles["c", a // 2] = big()
+            lo = 1024 * (a % 2)
+            return tiles["c", a // 2][:, lo : lo + 1024]
 
         def keep_prior(a):
-            if a % 2 == 0:
-                cov_sb[a // 2] = big()
-            nc.vector.tensor_tensor(
-                out=cov_sb[a // 2][:, 1024 * (a % 2) : 1024 * (a % 2) + 1024],
-                in0=prior_sb[:, a, :], in1=keep_all[:], op=ALU.mult,
-            )
+            nc.vector.tensor_tensor(out=cov_half(a), in0=prior_sb[:, a, :], in1=keep_all[:], op=ALU.mult)
 
-        def cov_tile(a, h):
-            b = bank()
+        def cov_rows(a):
             qs = slice(128 * a, 128 * a + 128)
-            for g in range(2):
-                nc.tensor.matmul_mx(
-                    out=b[:],
-                    lhsT=z_codes[g][:, qs].bitcast(FP8X4),
-                    lhsT_scale=z_scl[g][:, qs],
-                    rhs=em_codes[g][h][:].bitcast(FP8X4),
-                    rhs_scale=em_scl[g][h][:],
-                    start=(g == 0),
-                    stop=(g == 1),
-                )
-            lo = 1024 * (a % 2) + 512 * h
             view = "q (p u e) -> q p u e"
-            dst = cov_sb[a // 2][:, lo : lo + 512]
-            nc.vector.tensor_tensor(
-                out=dst.rearrange(view, u=2, e=2),
-                in0=b[:].rearrange("q (u p e) -> q p u e", u=2, e=2),
-                in1=dst.rearrange(view, u=2, e=2),
-                op=ALU.add,
-            )
-
-        def cov_store(a):
-            lo = 1024 * (a % 2)
-            nc.sync.dma_start(out=cov_view[:, a, :], in_=cov_sb[a // 2][:, lo : lo + 1024])
+            for h in range(2):
+                b = bank()
+                for g in range(2):
+                    nc.tensor.matmul_mx(
+                        out=b[:],
+                        lhsT=z_codes[g][:, qs].bitcast(FP8X4),
+                        lhsT_scale=z_scl[g][:, qs],
+                        rhs=em_codes[g][h][:].bitcast(FP8X4),
+                        rhs_scale=em_scl[g][h][:],
+                        start=(g == 0),
+                        stop=(g == 1),
+                    )
+                cols = slice(512 * h, 512 * h + 512)
+                dst = cov_half(a)[:, cols]
+                nc.vector.tensor_tensor(
+                    out=dst.rearrange(view, u=2, e=2),
+                    in0=b[:].rearrange("q (u p e) -> q p u e", u=2, e=2),
+                    in1=dst.rearrange(view, u=2, e=2),
+                    op=ALU.add,
+                )
+                nc.sync.dma_start(out=cov_view[:, a, cols], in_=dst)
 
         with tc.manual_schedule():
+            nc.vector.memset(ones[:], 1.0)
             nc.vector.memset(e_scale[:].rearrange("p g n -> p (g n)").bitcast(I32), 0)
             nc.vector.memset(keep_row[:], 0.0)
-            nc.vector.memset(ones[:], 1.0)
-            load_x(0)
-            load_prop(0, 0)
-            load_prop(1, 0)
-            load_x(1)
-            load_prop(2, 0)
-            load_prop(0, 1)
-            load_prop(1, 1)
+            load_x(2, 0)
+            load_x(2, 1)
             load_prop(2, 1)
-            load_y(0)
-            load_x(2)
-            load_y(1)
-            load(z_in[:], z_bytes.rearrange("(p a) m -> p a m", a=4))
+            x_transpose(2)
+            x_pull(2, 0)
+            load_x(1, 0)
+            x_pull(2, 1)
+            prop_interleave(2, 1)
+            load_prop(0, 1)
+            x_pull(2, 2)
+            x_quant(2, 1)
+            load_x(1, 1)
+            x_quant(2, 0)
+            prop_quant(2, 1)
+            load_prop(1, 1)
+            load_x(0, 0)
+            x_quant(2, 2)
+            x_transpose(1)
+            prop_interleave(0, 1)
+            load_x(0, 1)
+            prop_quant(0, 1)
+            x_pull(1, 0)
+            x_pull(1, 2)
+            prop_interleave(1, 1)
+            load_x(3, 0)
+            x_quant(1, 0)
+            x_transpose(0)
+            x_pull(1, 1)
+            load_x(3, 1)
+            x_pull(0, 0)
+            x_pull(0, 1)
+            load_prop(0, 0)
+            prop_quant(1, 1)
+            load_prop(1, 0)
+            x_quant(1, 1)
             load(z_sc[:], z_scale.rearrange("o (g p t) -> p (o g) t", g=2, t=4))
-            load(keep_row[0:1, :], keep.rearrange("(o n) -> o n", o=1))
-            load_e()
-            load_e_scales()
             load_y(2)
-
-            def p_quant(c, h, t):
-                quantize(p_codes[c][h][:], p_scl[c][h][:], t[:])
-
-            def x_q1(i, c, t):
-                quantize(x_codes[i][:, c, :], x_scl[i][:, c, :], t[:, :1024])
-
-            xb = x_transpose(0)
-            load_x(3)
-            load_y(3)
-            load(prior_sb[:], prior_view)
-            x0 = [pull_pairs(xb[0])]
-            p00 = prop_interleave(0, 0)
-            x0 += [pull_pairs(b) for b in xb[1:]]
-            x_q1(0, 0, x0[0])
-            p_quant(0, 0, p00)
-            p10 = prop_interleave(1, 0)
-            x_q1(0, 1, x0[1])
-            x_q1(0, 2, x0[2])
-            xb = x_transpose(1)
-            p_quant(1, 0, p10)
-            x1 = [pull_pairs(xb[0])]
-            p20 = prop_interleave(2, 0)
-            x1 += [pull_pairs(b) for b in xb[1:]]
-            f00 = [bank(), bank()]
-            for c in range(2):
-                for t in range(2):
-                    forecast_pass(0, t, 0, c, f00[t])
-            x_q1(1, 0, x1[0])
-            p_quant(2, 0, p20)
-            for t in range(2):
-                forecast_pass(0, t, 0, 2, f00[t])
-            x_q1(1, 1, x1[1])
-            p01 = prop_interleave(0, 1)
-            x_q1(1, 2, x1[2])
-            f10 = [forecast(1, t, 0) for t in range(2)]
-            p_quant(0, 1, p01)
-            p11 = prop_interleave(1, 1)
-            subtract(0, 0, 0, f00[0])
-            p_quant(1, 1, p11)
-            f01 = [bank(), bank()]
-            for c in range(2):
-                for t in range(2):
-                    forecast_pass(0, t, 1, c, f01[t])
-            p21 = prop_interleave(2, 1)
-            subtract(0, 1, 0, f00[1])
-            p_quant(2, 1, p21)
-            xb = x_transpose(2)
-            x2 = [pull_pairs(b) for b in xb]
-            for t in range(2):
-                forecast_pass(0, t, 1, 2, f01[t])
-            subtract(1, 0, 0, f10[0])
-            subtract(1, 1, 0, f10[1])
-            f11 = [forecast(1, t, 1) for t in range(2)]
-            for t in range(2):
-                subtract(0, t, 1, f01[t])
-            for c in range(3):
-                x_q1(2, c, x2[c])
-            z_widen(0)
+            x_quant(0, 0)
+            x_transpose(3)
+            load_prop(2, 0)
+            x_quant(1, 2)
+            x_quant(0, 1)
+            forecast0(1, 0)
+            forecast0(1, 1)
+            x_pull(0, 2)
+            x_pull(3, 0)
+            x_quant(0, 2)
+            x_pull(3, 2)
+            prop_interleave(0, 0)
+            prop_interleave(1, 0)
+            x_quant(3, 2)
+            forecast0(1, 2)
+            prop_quant(0, 0)
+            forecast(2, 1)
+            x_pull(3, 1)
+            load_y(0)
+            load(z_in[:], z_bytes.rearrange("(p a) m -> p a m", a=4))
+            prop_quant(1, 0)
+            prop_interleave(2, 0)
+            x_quant(3, 0)
+            prop_quant(2, 0)
+            forecast(1, 1)
+            subtract(0, 1)
+            forecast0(0, 0)
+            forecast0(0, 1)
+            forecast0(0, 2)
             z_widen(1)
-            for t in range(2):
-                subtract(1, t, 1, f11[t])
-            eb = [err_transpose(0, t) for t in range(2)]
-            e0 = [pull_pairs(b) for b in eb]
-            f20 = [forecast(2, t, 0) for t in range(2)]
-            mt = err_m_interleave(0, 0)
+            subtract(2, 1)
+            forecast(1, 0)
             z_widen(2)
+            x_quant(3, 1)
+            load_y(1)
             z_widen(3)
-            for t in range(2):
-                err_t_quant(0, t, e0[t])
-            eb = [err_transpose(1, t) for t in range(2)]
-            e1 = [pull_pairs(b) for b in eb]
-            err_m_quant(0, 0, mt)
-            for t in range(2):
-                subtract(2, t, 0, f20[t])
-            maps_unit(0, 0, (3,), 2)
-            for t in range(2):
-                err_t_quant(1, t, e1[t])
-            mt = err_m_interleave(0, 1)
-            zt = [grouped() for g in range(2)]
-            zb = [z_transpose(g, 0) for g in range(2)]
-            err_m_quant(0, 1, mt)
-            maps_unit(0, 1, (), 2)
-            for g in range(2):
-                z_pull(g, 0, zb[g], zt[g])
-            f21 = [forecast(2, t, 1) for t in range(2)]
-            for t in range(2):
-                subtract(2, t, 1, f21[t])
+            subtract(1, 1)
+            forecast(2, 0)
+            subtract(1, 0)
+            subtract(0, 0)
+            forecast(3, 0)
+            err_transpose(0)
+            load(keep_row[0:1, :], keep.rearrange("(o n) -> o n", o=1))
+            subtract(2, 0)
+            load_y(3)
+            z_widen(0)
+            load_e()
+            err_pull(0)
+            err_transpose(1)
+            err_pull(1)
+            load_e_scales()
+            subtract(3, 0)
+            err_transpose(2)
+            load(prior_sb[:], prior_view)
+            forecast(3, 1)
+            err_quant(0)
+            err_pull(2)
+            err_quant(1)
+            month_interleave(0, 0)
+            subtract(3, 1)
             keep_spread()
-            xb = x_transpose(3)
-            x3 = [pull_pairs(b) for b in xb]
-            eb = [err_transpose(2, t) for t in range(2)]
-            for c in range(3):
-                x_q1(3, c, x3[c])
-            e2 = [pull_pairs(b) for b in eb]
+            maps_half(1, 1, 0)
+            err_quant(2)
+            maps_half(1, 0, 1)
+            month_interleave(0, 1)
+            maps_half(0, 0, 1)
             keep_prior(0)
-            maps_unit(1, 0, (), 2)
-            for t in range(2):
-                err_t_quant(2, t, e2[t])
-            keep_prior(1)
-            f30 = [forecast(3, t, 0) for t in range(2)]
-            for t in range(2):
-                subtract(3, t, 0, f30[t])
-            f31 = [forecast(3, t, 1) for t in range(2)]
-            mt = err_m_interleave(1, 0)
-            for t in range(2):
-                subtract(3, t, 1, f31[t])
-            maps_unit(1, 1, (), 2)
-            err_m_quant(1, 0, mt)
-            zb = [z_transpose(g, 1) for g in range(2)]
-            eb = [err_transpose(3, t) for t in range(2)]
-            e3 = [pull_pairs(b) for b in eb]
-            for g in range(2):
-                z_pull(g, 1, zb[g], zt[g])
-            mt = err_m_interleave(1, 1)
-            for g in range(2):
-                quantize(z_codes[g][:], z_scl[g][:], zt[g][:])
-            maps_unit(2, 0, (), 2)
-            err_m_quant(1, 1, mt)
-            for t in range(2):
-                err_t_quant(3, t, e3[t])
-            maps_unit(2, 1, (), 2)
-            for a in range(2):
-                for h in range(2):
-                    cov_tile(a, h)
-                cov_store(a)
-            keep_prior(2)
+            month_quant(0, 0)
+            maps_half(1, 1, 1)
+            maps_half(0, 1, 0)
+            month_interleave(1, 0)
+            month_quant(0, 1)
+            maps_half(0, 0, 0)
+            err_transpose(3)
+            z_transpose(1)
+            z_pull(1)
+            err_pull(3)
+            maps_half(2, 0, 1)
+            err_quant(3)
+            maps_half(1, 0, 0)
             keep_prior(3)
-            maps_unit(3, 0, (), 2)
-            for a in range(2, 4):
-                for h in range(2):
-                    cov_tile(a, h)
-                cov_store(a)
-            maps_unit(3, 1, (3,), 4)
+            maps_half(2, 0, 0)
+            maps_half(0, 1, 1)
+            maps_half(3, 0, 0)
+            month_interleave(1, 1)
+            month_quant(1, 0)
+            keep_prior(2)
+            maps_half(2, 1, 1)
+            maps_half(2, 1, 0)
+            month_quant(1, 1)
+            z_transpose(0)
+            maps_half(3, 1, 0)
+            maps_half(3, 0, 1)
+            z_pull(0)
+            z_quant()
+            maps_half(3, 1, 1)
+            keep_prior(1)
+            cov_rows(3)
+            cov_rows(2)
+            cov_rows(0)
+            cov_rows(1)

from contextlib import ExitStack

import concourse.mybir as mybir
from concourse.masks import make_identity

M, K, N, R, Q = 1024, 1536, 1024, 2048, 512
FLOPS = 2 * (M * K * N + M * N * R + Q * M * N)

F32 = mybir.dt.float32
BF16 = mybir.dt.bfloat16
U32 = mybir.dt.uint32
I32 = mybir.dt.int32
U8 = mybir.dt.uint8
FP8 = mybir.dt.float8_e4m3fn
FP8X4 = mybir.dt.float8_e4m3fn_x4
FP4X4 = mybir.dt.float4_e2m1fn_x4
ALU = mybir.AluOpType

P = 128
BANK = 512
KP = K // 512
PAIRS = 4
MAPS_ON_VECTOR = {}
LAST = (3, 1)
V_COLS = 336


def tile_lim_error_update_s8_kernel(tc, x, prop, y, eof_words, eof_scales, z_bytes, z_scale, prior, keep, maps, cov):
    nc = tc.nc
    with ExitStack() as ctx:
        keepers = ctx.enter_context(tc.tile_pool(name="keepers", bufs=1))
        work = ctx.enter_context(tc.tile_pool(name="work", bufs=2))
        psum = ctx.enter_context(tc.psum_pool(name="psum", bufs=8))

        def kept(name, shape, dt):
            return keepers.tile(shape, dt, name=name, align_bytes=64)

        def bank(name="bank"):
            return psum.tile([P, BANK], F32, name="bank")

        def big():
            return work.tile([P, 2048], F32, name="big", bufs=7, align_bytes=64)

        def grouped():
            return work.tile([P, 2048], BF16, name="grouped", bufs=5, align_bytes=64)

        def half():
            return work.tile([P, 1024], BF16, name="half", bufs=7, align_bytes=64)

        ident = kept("ident", [P, P], F32)
        make_identity(nc, ident[:])
        ones = kept("ones", [P, BANK], BF16)
        keep_row = kept("keep_row", [P, N], BF16)
        e_scale = kept("e_scale", [P, 2, R], U8)

        x_view = x.rearrange("(g p t) k -> g p t k", g=2, t=4)
        y_view = y.rearrange("(g p t) n -> g p t n", g=2, t=4)
        maps_view = maps.rearrange("(g p t) r -> g p t r", g=2, t=4)
        prop_view = prop.rearrange("(c p j) n -> c p j n", p=P, j=4)
        prior_view = prior.rearrange("(p a) n -> p a n", a=4)
        cov_view = cov.rearrange("(p a) n -> p a n", a=4)

        x_raw, y_raw, prop_raw = {}, {}, {}
        x_codes = [kept("x_codes%d" % i, [P, KP, 256], U32) for i in range(PAIRS)]
        x_scl = [kept("x_scl%d" % i, [P, KP, 256], U8) for i in range(PAIRS)]
        p_codes = [[kept("p_codes%d%d" % (c, h), [P, 512], U32) for h in range(2)] for c in range(KP)]
        p_scl = [[kept("p_scl%d%d" % (c, h), [P, 512], U8) for h in range(2)] for c in range(KP)]
        err = [[kept("err%d%d" % (g, h), [P, 4, 512], BF16) for h in range(2)] for g in range(2)]
        et_codes = [kept("et_codes%d" % i, [P, 2, 256], U32) for i in range(PAIRS)]
        et_scl = [kept("et_scl%d" % i, [P, 2, 256], U8) for i in range(PAIRS)]
        em_codes = [[kept("em_codes%d%d" % (g, h), [P, 512], U32) for h in range(2)] for g in range(2)]
        em_scl = [[kept("em_scl%d%d" % (g, h), [P, 512], U8) for h in range(2)] for g in range(2)]
        z_codes = [kept("z_codes%d" % g, [P, Q], U32) for g in range(2)]
        z_scl = [kept("z_scl%d" % g, [P, Q], U8) for g in range(2)]
        e_words = kept("e_words", [P, 2, 2 * R], U8)
        z_in = kept("z_in", [P, 4, M], U8)
        z_sc = kept("z_sc", [P, 2, 4], F32)
        z_wide = kept("z_wide", [P, 4, M], BF16)
        prior_sb = kept("prior_sb", [P, 4, N], BF16)
        keep_all = kept("keep_all", [P, N], F32)

        def load(out, in_):
            nc.sync.dma_start(out=out, in_=in_)

        def load_x(i, t):
            g, h = divmod(i, 2)
            if t == 0:
                x_raw[i] = work.tile([P, 2, K], BF16, name="x_raw", bufs=3, align_bytes=64)
            load(x_raw[i][:, t, :], x_view[g][:, 2 * h + t, :])

        def load_y(i):
            g, h = divmod(i, 2)
            if h == 0:
                y_raw[g] = kept("y_raw%d" % g, [P, 4, N], BF16)
            load(y_raw[g][:, 2 * h : 2 * h + 2, :], y_view[g][:, 2 * h : 2 * h + 2, :])

        def load_prop(c, h):
            if c not in prop_raw:
                prop_raw[c] = big()[:].bitcast(BF16).rearrange("p (j n) -> p j n", j=4)
            cols = slice(512 * h, 512 * h + 512)
            load(prop_raw[c][:, :, cols], prop_view[c][:, :, cols])

        def load_e():
            load(e_words[:].bitcast(I32), eof_words.rearrange("g p b -> p g b").bitcast(I32))

        def load_e_scales():
            for q in range(4):
                load(
                    e_scale[32 * q : 32 * q + 4, :, :].bitcast(I32),
                    eof_scales[:, 4 * q : 4 * q + 4, :].rearrange("g q n -> q g n").bitcast(I32),
                )

        banks, tiles = {}, {}

        def quantize(codes, scl, t):
            nc.vector.quantize_mx(out=codes.bitcast(FP8X4), scales=scl, in_=t)

        def warm(n):
            b = bank()
            for k in range(n):
                nc.tensor.matmul(b[:], ones[:, :P], ones[:], start=True, stop=True)

        def prop_interleave(c, h):
            t = tiles["prop", c, h] = grouped()
            dst = t[:].rearrange("p (n j) -> p n j", j=4)
            src = prop_raw[c][:, :, 512 * h : 512 * h + 512].rearrange("p j n -> p n j")
            nc.scalar.copy(out=dst[:, V_COLS:, :], in_=src[:, V_COLS:, :])
            nc.vector.tensor_copy(out=dst[:, :V_COLS, :], in_=src[:, :V_COLS, :])

        def prop_quant(c, h):
            quantize(p_codes[c][h][:], p_scl[c][h][:], tiles["prop", c, h][:])

        def x_transpose(i):
            for c in range(KP):
                banks["x", i, c] = bank()
            for t in range(2):
                words = x_raw[i][:, t, :].bitcast(F32)
                for c in range(KP):
                    v = banks["x", i, c][:].rearrange("p (u t m) -> p u t m", u=2, t=2)
                    for u in range(2):
                        nc.tensor.transpose(v[:, u, t, :], words[:, 256 * c + u : 256 * (c + 1) : 2], ident[:])

        def pull_words(b):
            t = half()
            nc.scalar.copy(
                out=t[:].bitcast(F32).rearrange("p (m u) -> p m u", u=2),
                in_=b[:].rearrange("p (u m) -> p m u", u=2),
            )
            return t

        def x_pull(i, c):
            tiles["x", i, c] = pull_words(banks["x", i, c])

        def x_quant(i, c):
            quantize(x_codes[i][:, c, :], x_scl[i][:, c, :], tiles["x", i, c][:])

        def forecast_pass(i, t, h, c):
            cols = slice(128 * t, 128 * t + 128)
            if c == 0:
                banks["f", i, t, h] = bank()
            nc.tensor.matmul_mx(
                out=banks["f", i, t, h][:],
                lhsT=x_codes[i][:, c, cols].bitcast(FP8X4),
                lhsT_scale=x_scl[i][:, c, cols],
                rhs=p_codes[c][h][:].bitcast(FP8X4),
                rhs_scale=p_scl[c][h][:],
                start=(c == 0),
                stop=(c == KP - 1),
            )

        def forecast0(h, c):
            for t in range(2):
                forecast_pass(0, t, h, c)

        def forecast(i, h):
            for t in range(2):
                for c in range(KP):
                    forecast_pass(i, t, h, c)

        def subtract(i, h):
            g, tp = divmod(i, 2)
            view = "m (p u e) -> m u p e"
            for t in range(2):
                tt = 2 * tp + t
                nc.vector.tensor_tensor(
                    out=err[g][h][:, tt, :].rearrange("m (u p e) -> m u p e", u=2, e=2),
                    in0=y_raw[g][:, tt, 512 * h : 512 * h + 512].rearrange(view, u=2, e=2),
                    in1=banks["f", i, t, h][:].rearrange(view, u=2, e=2),
                    op=ALU.subtract,
                )

        def err_transpose(i):
            g, tp = divmod(i, 2)
            for t in range(2):
                b = banks["e", i, t] = bank()
                v = b[:].rearrange("p (u h m) -> p u h m", u=2, h=2)
                for h in range(2):
                    words = err[g][h][:, 2 * tp + t, :].bitcast(F32)
                    for u in range(2):
                        nc.tensor.transpose(v[:, u, h, :], words[:, 128 * u : 128 * u + 128], ident[:])

        def err_pull(i):
            for t in range(2):
                tiles["e", i, t] = pull_words(banks["e", i, t])

        def err_quant(i):
            for t in range(2):
                quantize(et_codes[i][:, t, :], et_scl[i][:, t, :], tiles["e", i, t][:])

        def month_interleave(g, h):
            t = tiles["m", g, h] = grouped()
            nc.vector.tensor_copy(
                out=t[:].rearrange("p (n j) -> p n j", j=4), in_=err[g][h][:].rearrange("p j n -> p n j")
            )

        def month_quant(g, h):
            quantize(em_codes[g][h][:], em_scl[g][h][:], tiles["m", g, h][:])

        def maps_half(i, t, j):
            g, tp = divmod(i, 2)
            if ("o", i, t) not in tiles:
                tiles["o", i, t] = big()
            o = tiles["o", i, t]
            for r in (2 * j, 2 * j + 1):
                b = bank()
                for h in range(2):
                    k = slice(128 * h, 128 * h + 128)
                    nc.tensor.matmul_mx(
                        out=b[:],
                        lhsT=et_codes[i][:, t, k].bitcast(FP8X4),
                        lhsT_scale=et_scl[i][:, t, k],
                        rhs=e_words[:, h, 1024 * r : 1024 * r + 1024].bitcast(FP4X4),
                        rhs_scale=e_scale[:, h, 512 * r : 512 * r + 512],
                        start=(h == 0),
                        stop=(h == 1),
                    )
                cols = slice(512 * r, 512 * r + 512)
                if (i, t, r) in MAPS_ON_VECTOR:
                    nc.vector.tensor_copy(out=o[:, cols], in_=b[:])
                else:
                    nc.scalar.copy(out=o[:, cols], in_=b[:])
                if (i, t) == LAST:
                    nc.sync.dma_start(out=maps_view[g][:, 2 * tp + t, cols], in_=o[:, cols])
            if (i, t) != LAST:
                cols = slice(1024 * j, 1024 * j + 1024)
                nc.sync.dma_start(out=maps_view[g][:, 2 * tp + t, cols], in_=o[:, cols])

        def z_widen(a):
            nc.scalar.copy(out=z_wide[:, a, :], in_=z_in[:, a, :].bitcast(FP8))

        def z_transpose(ap):
            for g in range(2):
                b = banks["z", g, ap] = bank()
                v = b[:].rearrange("p (u a q) -> p u a q", u=2, a=2)
                for u in range(2):
                    for a in range(2):
                        words = z_wide[:, 2 * ap + a, :].bitcast(F32)
                        nc.tensor.transpose(v[:, u, a, :], words[:, 256 * g + u : 256 * (g + 1) : 2], ident[:])

        def z_pull(ap):
            for g in range(2):
                if ("z", g) not in tiles:
                    tiles["z", g] = grouped()
                nc.vector.tensor_tensor(
                    out=tiles["z", g][:, 1024 * ap : 1024 * ap + 1024].rearrange("p (q u e) -> p q u e", u=2, e=2),
                    in0=banks["z", g, ap][:].bitcast(BF16).rearrange("p (u q e) -> p q u e", u=2, e=2),
                    in1=z_sc[:, g, :].rearrange("p (u e) -> p u e", u=2).unsqueeze(1).to_broadcast([P, 256, 2, 2]),
                    op=ALU.mult,
                )

        def z_quant():
            for g in range(2):
                quantize(z_codes[g][:], z_scl[g][:], tiles["z", g][:])

        def keep_spread():
            for h in range(2):
                b = bank()
                cols = slice(512 * h, 512 * h + 512)
                nc.tensor.matmul(b[:], ones[:, :P], keep_row[:, cols], start=True, stop=True)
                nc.scalar.copy(out=keep_all[:, cols], in_=b[:])

        def cov_half(a):
            if ("c", a // 2) not in tiles:
                tiles["c", a // 2] = big()
            lo = 1024 * (a % 2)
            return tiles["c", a // 2][:, lo : lo + 1024]

        def keep_prior(a):
            nc.vector.tensor_tensor(out=cov_half(a), in0=prior_sb[:, a, :], in1=keep_all[:], op=ALU.mult)

        def cov_rows(a):
            qs = slice(128 * a, 128 * a + 128)
            view = "q (p u e) -> q p u e"
            for h in range(2):
                b = bank()
                for g in range(2):
                    nc.tensor.matmul_mx(
                        out=b[:],
                        lhsT=z_codes[g][:, qs].bitcast(FP8X4),
                        lhsT_scale=z_scl[g][:, qs],
                        rhs=em_codes[g][h][:].bitcast(FP8X4),
                        rhs_scale=em_scl[g][h][:],
                        start=(g == 0),
                        stop=(g == 1),
                    )
                cols = slice(512 * h, 512 * h + 512)
                dst = cov_half(a)[:, cols]
                nc.vector.tensor_tensor(
                    out=dst.rearrange(view, u=2, e=2),
                    in0=b[:].rearrange("q (u p e) -> q p u e", u=2, e=2),
                    in1=dst.rearrange(view, u=2, e=2),
                    op=ALU.add,
                )
                nc.sync.dma_start(out=cov_view[:, a, cols], in_=dst)

        with tc.manual_schedule():
            nc.vector.memset(ones[:], 1.0)
            nc.vector.memset(e_scale[:].rearrange("p g n -> p (g n)").bitcast(I32), 0)
            nc.vector.memset(keep_row[:], 0.0)
            load_x(2, 0)
            load_x(2, 1)
            load_prop(2, 1)
            x_transpose(2)
            x_pull(2, 0)
            load_x(1, 0)
            x_pull(2, 1)
            prop_interleave(2, 1)
            load_prop(0, 1)
            x_pull(2, 2)
            x_quant(2, 1)
            load_x(1, 1)
            x_quant(2, 0)
            prop_quant(2, 1)
            load_prop(1, 1)
            load_x(0, 0)
            x_quant(2, 2)
            x_transpose(1)
            prop_interleave(0, 1)
            load_x(0, 1)
            prop_quant(0, 1)
            x_pull(1, 0)
            x_pull(1, 2)
            prop_interleave(1, 1)
            load_x(3, 0)
            x_quant(1, 0)
            x_transpose(0)
            x_pull(1, 1)
            load_x(3, 1)
            x_pull(0, 0)
            x_pull(0, 1)
            load_prop(0, 0)
            prop_quant(1, 1)
            load_prop(1, 0)
            x_quant(1, 1)
            load(z_sc[:], z_scale.rearrange("o (g p t) -> p (o g) t", g=2, t=4))
            load_y(2)
            x_quant(0, 0)
            x_transpose(3)
            load_prop(2, 0)
            x_quant(1, 2)
            x_quant(0, 1)
            forecast0(1, 0)
            forecast0(1, 1)
            x_pull(0, 2)
            x_pull(3, 0)
            x_quant(0, 2)
            x_pull(3, 2)
            prop_interleave(0, 0)
            prop_interleave(1, 0)
            x_quant(3, 2)
            forecast0(1, 2)
            prop_quant(0, 0)
            forecast(2, 1)
            x_pull(3, 1)
            load_y(0)
            load(z_in[:], z_bytes.rearrange("(p a) m -> p a m", a=4))
            prop_quant(1, 0)
            prop_interleave(2, 0)
            x_quant(3, 0)
            prop_quant(2, 0)
            forecast(1, 1)
            subtract(0, 1)
            forecast0(0, 0)
            forecast0(0, 1)
            forecast0(0, 2)
            z_widen(1)
            subtract(2, 1)
            forecast(1, 0)
            z_widen(2)
            x_quant(3, 1)
            load_y(1)
            z_widen(3)
            subtract(1, 1)
            forecast(2, 0)
            subtract(1, 0)
            subtract(0, 0)
            forecast(3, 0)
            err_transpose(0)
            load(keep_row[0:1, :], keep.rearrange("(o n) -> o n", o=1))
            subtract(2, 0)
            load_y(3)
            z_widen(0)
            load_e()
            err_pull(0)
            err_transpose(1)
            err_pull(1)
            load_e_scales()
            subtract(3, 0)
            err_transpose(2)
            load(prior_sb[:], prior_view)
            forecast(3, 1)
            err_quant(0)
            err_pull(2)
            err_quant(1)
            month_interleave(0, 0)
            subtract(3, 1)
            keep_spread()
            maps_half(1, 1, 0)
            err_quant(2)
            maps_half(1, 0, 1)
            month_interleave(0, 1)
            maps_half(0, 0, 1)
            keep_prior(0)
            month_quant(0, 0)
            maps_half(1, 1, 1)
            maps_half(0, 1, 0)
            month_interleave(1, 0)
            month_quant(0, 1)
            maps_half(0, 0, 0)
            err_transpose(3)
            z_transpose(1)
            z_pull(1)
            err_pull(3)
            maps_half(2, 0, 1)
            err_quant(3)
            maps_half(1, 0, 0)
            keep_prior(3)
            maps_half(2, 0, 0)
            maps_half(0, 1, 1)
            maps_half(3, 0, 0)
            month_interleave(1, 1)
            month_quant(1, 0)
            keep_prior(2)
            maps_half(2, 1, 1)
            maps_half(2, 1, 0)
            month_quant(1, 1)
            z_transpose(0)
            maps_half(3, 1, 0)
            maps_half(3, 0, 1)
            z_pull(0)
            z_quant()
            maps_half(3, 1, 1)
            keep_prior(1)
            cov_rows(3)
            cov_rows(2)
            cov_rows(0)
            cov_rows(1)
